import numpy as np
import ml_dtypes


def mxq(x, axis, fmt="e4m3"):
    dtype, down = {"e4m3": (ml_dtypes.float8_e4m3fn, 7), "e5m2": (ml_dtypes.float8_e5m2, 14)}[fmt]
    v = np.moveaxis(np.asarray(x, np.float32).astype(ml_dtypes.bfloat16).astype(np.float64), axis, -1)
    blocks = v.reshape(v.shape[:-1] + (-1, 32))
    amax = np.abs(blocks).max(-1, keepdims=True)
    byte = np.maximum(np.where(amax > 0, np.frexp(amax)[1] - 1 + 127, 0) - down, 1)
    scale = np.exp2(byte - 127.0)
    codes = (blocks / scale).astype(np.float32).astype(dtype).astype(np.float64)
    return np.moveaxis((codes * scale).reshape(v.shape), -1, axis)


WIDE = False


def mx_kscale(k):
    if not WIDE:
        return np.ones(k)
    levels = np.array([10, -10, 5, -5, 0])
    if k % 512:
        return np.exp2(np.random.permutation(np.resize(levels, k // 32))).repeat(32)
    a = np.empty((k // 512, 16))
    for p in range(k // 512):
        a[p, :8] = np.random.permutation(np.resize(levels, 8))
        for g in range(8):
            far = levels[np.abs(levels - a[p, g]) >= 10]
            a[p, g + 8] = far[np.random.randint(len(far))]
    return np.exp2(a.ravel()).repeat(32)


def f64(x):
    return np.asarray(x).astype(np.float64)


def striped8(idx):
    return np.asarray(idx).reshape(8, -1, 16).transpose(0, 2, 1).reshape(128, -1).astype(np.uint16)


def unstriped8(offs):
    return offs.reshape(8, 16, -1).transpose(0, 2, 1).reshape(8, -1).astype(np.int64)


def pick8(x, idx, run):
    r = np.arange(len(x))
    return x[r[:, None], idx[r % (8 * run) // run]]


E2M1 = np.array([0.0, 0.5, 1.0, 1.5, 2.0, 3.0, 4.0, 6.0, -0.0, -0.5, -1.0, -1.5, -2.0, -3.0, -4.0, -6.0])


def pack_weight(w, fmt):
    k, n = w.shape
    w = f64(np.asarray(w, np.float32).astype(ml_dtypes.bfloat16)).reshape(k // 32, 32, n)
    amax = np.abs(w).max(1)
    if fmt == "e4m3":
        byte = np.frexp(amax)[1] - 1 + 127 - 7
    else:
        mant, ex = np.frexp(amax / 6.0)
        byte = np.where(mant > 0.5, ex, ex - 1) + 127
    byte = np.clip(np.where(amax > 0, byte, 1), 1, 254)
    scaled = (w * np.exp2(127.0 - byte)[:, None, :]).reshape(k, n).astype(np.float32)
    by_word = np.ascontiguousarray(scaled.reshape(k // 512, 128, 4, n).transpose(0, 1, 3, 2))
    if fmt == "e4m3":
        words = by_word.astype(ml_dtypes.float8_e4m3fn).view(np.uint8)
    else:
        c = by_word.astype(ml_dtypes.float4_e2m1fn).view(np.uint8) & 0xF
        words = (c[..., 0::2] | (c[..., 1::2] << 4)).reshape(k // 512, 128, 2 * n)
    return np.ascontiguousarray(words), np.ascontiguousarray(byte.astype(np.uint8).reshape(k // 512, 16, n))


def unpack_weight(words, scales, fmt):
    g, _, n = scales.shape
    words = np.ascontiguousarray(words).reshape(g, 128, n, -1)
    if fmt == "e4m3":
        vals = words.view(ml_dtypes.float8_e4m3fn).astype(np.float64)
    else:
        nib = np.empty((g, 128, n, 4), np.uint8)
        nib[..., 0::2] = words & 0xF
        nib[..., 1::2] = words >> 4
        vals = E2M1[nib]
    vals = vals * np.repeat(np.exp2(scales.astype(np.float64) - 127.0), 8, axis=1)[..., None]
    return vals.transpose(0, 1, 3, 2).reshape(g * 512, n)


def sigmoid(v):
    return 1.0 / (1.0 + np.exp(-v))


D, T, I, Q = 512, 1024, 512, 128


def setup_inputs():
    n = np.random.standard_normal
    idx = np.stack([np.random.permutation(T)[:I] for _ in range(8)])
    idx2 = np.stack([np.random.permutation(T)[:I] for _ in range(8)])
    idx3 = np.stack([np.random.permutation(T)[:I] for _ in range(8)])
    fd = mx_kscale(D)
    keysp = pack_weight(n((D, T)) / fd[:, None], "e4m3")
    tagsp = pack_weight(n((D, T)) / fd[:, None], "e2m1")
    return {
        "query": (n((D, Q)) * 0.75 / np.sqrt(D) * fd[:, None]).astype(np.float32),
        "query2": (n((D, Q)) * 0.75 / np.sqrt(D) * fd[:, None]).astype(np.float32),
        "keys_words": keysp[0],
        "keys_scales": keysp[1],
        "tags_words": tagsp[0],
        "tags_scales": tagsp[1],
        "thr": (np.random.uniform(-0.6, 0.6, (Q, 1))).astype(np.float32),
        "slope": (np.random.uniform(1.0, 3.0, (Q, 1))).astype(np.float32),
        "offs": striped8(idx),
        "offs2": striped8(idx2),
        "offs3": striped8(idx3),
    }


def reference(query, query2, keys_words, keys_scales, tags_words, tags_scales, thr, slope, offs, offs2, offs3):
    idx = unstriped8(offs)
    idx2 = unstriped8(offs2)
    idx3 = unstriped8(offs3)
    keysu = unpack_weight(keys_words, keys_scales, "e4m3")
    tagsu = unpack_weight(tags_words, tags_scales, "e2m1")
    queryq = mxq(f64(query), 0, "e4m3")
    query2q = mxq(f64(query2), 0, "e4m3")
    a = queryq.T @ keysu + query2q.T @ tagsu
    s1 = sigmoid(pick8(a, idx, 16) * f64(slope) + f64(thr))
    f1 = np.zeros((Q, T))
    f1[np.arange(Q)[:, None], idx2[np.arange(Q) % 128 // 16]] = s1
    cc = a + f1 * 2.0
    y = pick8(cc, idx3, 16)
    return y

@@ -1,0 +1,128 @@
+from contextlib import ExitStack
+
+import concourse.mybir as mybir
+
+D, T, SLOTS, Q = 512, 1024, 512, 128
+FLOPS = 2 * 2 * D * Q * T
+
+F32 = mybir.dt.float32
+BF16 = mybir.dt.bfloat16
+I32 = mybir.dt.int32
+U32 = mybir.dt.uint32
+U16 = mybir.dt.uint16
+U8 = mybir.dt.uint8
+FP8X4 = mybir.dt.float8_e4m3fn_x4
+FP4X4 = mybir.dt.float4_e2m1fn_x4
+ALU = mybir.AluOpType
+ACT = mybir.ActivationFunctionType
+
+P = 128
+PACK = 4
+BANKS = 4
+N = T // BANKS
+HALF = SLOTS // 2
+LIST_COLS = SLOTS // 16
+HALF_COLS = LIST_COLS // 2
+
+
+def load_scale_rows(queue, plane, rows):
+    words = rows[0].bitcast(I32)
+    for quad in range(4):
+        queue.dma_start(
+            out=plane[32 * quad : 32 * quad + 4, :].bitcast(I32),
+            in_=words[4 * quad : 4 * quad + 4, :],
+        )
+
+
+def tile_attend_openings_parts_kernel(
+    tc, query, query2, keys_words, keys_scales, tags_words, tags_scales, thr, slope, offs, offs2, offs3, out
+):
+    nc = tc.nc
+    with ExitStack() as ctx:
+        sb = ctx.enter_context(tc.tile_pool(name="sb", bufs=1))
+        psum = ctx.enter_context(tc.psum_pool(name="psum", bufs=1))
+
+        tag_plane = sb.tile([P, T], U8, align_bytes=64)
+        key_plane = sb.tile([P, T], U8, align_bytes=64)
+        gates = sb.tile([P, T], F32)
+        nc.vector.memset(tag_plane[:].bitcast(I32), 0)
+        nc.vector.memset(key_plane[:].bitcast(I32), 0)
+        nc.vector.memset(gates[:], 0.0)
+
+        q2_raw = sb.tile([P, PACK, Q], F32)
+        q1_raw = sb.tile([P, PACK, Q], F32)
+        tag_codes = sb.tile([P, 2 * T], U8, align_bytes=64)
+        key_codes = sb.tile([P, T], U32, align_bytes=64)
+        thr_sb = sb.tile([P, 1], F32)
+        slope_sb = sb.tile([P, 1], F32)
+        open_list = sb.tile([P, LIST_COLS], U16)
+        place_list = sb.tile([P, LIST_COLS], U16)
+        read_list = sb.tile([P, LIST_COLS], U16)
+
+        nc.sync.dma_start(out=q2_raw[:], in_=query2.rearrange("(p j) q -> p j q", j=PACK))
+        nc.sync.dma_start(out=q1_raw[:], in_=query.rearrange("(p j) q -> p j q", j=PACK))
+        load_scale_rows(nc.scalar, tag_plane, tags_scales)
+        nc.sync.dma_start(out=tag_codes[:].bitcast(I32), in_=tags_words[0].bitcast(I32))
+        nc.sync.dma_start(
+            out=key_codes[:].bitcast(I32), in_=keys_words[0].rearrange("p n t -> p (n t)").bitcast(I32)
+        )
+        load_scale_rows(nc.scalar, key_plane, keys_scales)
+        nc.gpsimd.dma_start(out=slope_sb[:], in_=slope)
+        nc.gpsimd.dma_start(out=thr_sb[:], in_=thr)
+        nc.sync.dma_start(open_list[:], offs)
+        nc.sync.dma_start(place_list[:], offs2)
+        nc.sync.dma_start(read_list[:], offs3)
+
+        quantised = []
+        for name, raw in (("q2", q2_raw), ("q1", q1_raw)):
+            grouped = sb.tile([P, Q, PACK], BF16, align_bytes=64, name=name + "_grouped")
+            codes = sb.tile([P, Q], U32, align_bytes=64, name=name + "_codes")
+            scales = sb.tile([P, Q], U8, align_bytes=64, name=name + "_scales")
+            nc.vector.tensor_copy(out=grouped[:], in_=raw[:].rearrange("p j q -> p q j"))
+            nc.vector.quantize_mx(
+                out=codes[:].bitcast(FP8X4), scales=scales[:], in_=grouped[:].rearrange("p q j -> p (q j)")
+            )
+            quantised.append((codes, scales))
+        (q2_codes, q2_scales), (q1_codes, q1_scales) = quantised
+
+        banks = [psum.tile([P, N], F32, name="bank%d" % b) for b in range(BANKS)]
+        for b in range(BANKS):
+            nc.tensor.matmul_mx(
+                out=banks[b][:],
+                lhsT=q2_codes[:].bitcast(FP8X4),
+                lhsT_scale=q2_scales[:],
+                rhs=tag_codes[:, 2 * N * b : 2 * N * (b + 1)].bitcast(FP4X4),
+                rhs_scale=tag_plane[:, N * b : N * (b + 1)],
+                start=True,
+                stop=False,
+            )
+        scores = sb.tile([P, T], F32)
+        for b in range(BANKS):
+            nc.tensor.matmul_mx(
+                out=banks[b][:],
+                lhsT=q1_codes[:].bitcast(FP8X4),
+                lhsT_scale=q1_scales[:],
+                rhs=key_codes[:, N * b : N * (b + 1)].bitcast(FP8X4),
+                rhs_scale=key_plane[:, N * b : N * (b + 1)],
+                start=False,
+                stop=True,
+            )
+            nc.vector.tensor_copy(out=scores[:, N * b : N * (b + 1)], in_=banks[b][:])
+
+        for h in range(2):
+            cols = slice(h * HALF_COLS, (h + 1) * HALF_COLS)
+            opened = sb.tile([P, HALF], F32, name="opened%d" % h)
+            nc.scalar.activation(
+                opened[:], scores[:].indirect(open_list[:, cols]), ACT.Sigmoid, bias=thr_sb[:], scale=slope_sb[:]
+            )
+            nc.vector.tensor_copy(gates[:].indirect(place_list[:, cols]), opened[:])
+
+        gated = sb.tile([P, T], F32)
+        nc.vector.scalar_tensor_tensor(gated[:], gates[:], 2.0, scores[:], ALU.mult, ALU.add)
+
+        first = sb.tile([P, HALF], F32)
+        second = sb.tile([P, HALF], F32)
+        nc.vector.tensor_copy(first[:], gated[:].indirect(read_list[:, 0:HALF_COLS]))
+        nc.scalar.activation(second[:], gated[:].indirect(read_list[:, HALF_COLS:LIST_COLS]), ACT.Copy)
+        nc.sync.dma_start(out=out[:, 0:HALF], in_=first[:])
+        nc.scalar.dma_start(out=out[:, HALF:SLOTS], in_=second[:])

@@ -18,8 +18,8 @@ ACT = mybir.ActivationFunctionType
 
 P = 128
 PACK = 4
-BANKS = 4
-N = T // BANKS
+BANK_COLS = ((0, 256), (256, 512), (512, 768), (768, 896), (896, 1024))
+POOL_FROM = 768
 HALF = SLOTS // 2
 LIST_COLS = SLOTS // 16
 HALF_COLS = LIST_COLS // 2
@@ -45,14 +45,12 @@ def tile_attend_openings_parts_kernel(
         tag_plane = sb.tile([P, T], U8, align_bytes=64)
         key_plane = sb.tile([P, T], U8, align_bytes=64)
         gates = sb.tile([P, T], F32)
-        nc.vector.memset(tag_plane[:].bitcast(I32), 0)
-        nc.vector.memset(key_plane[:].bitcast(I32), 0)
         nc.vector.memset(gates[:], 0.0)
 
         q2_raw = sb.tile([P, PACK, Q], F32)
         q1_raw = sb.tile([P, PACK, Q], F32)
         tag_codes = sb.tile([P, 2 * T], U8, align_bytes=64)
-        key_codes = sb.tile([P, T], U32, align_bytes=64)
+        key_codes = [sb.tile([P, T // 2], U32, align_bytes=64, name="key_codes%d" % h) for h in range(2)]
         thr_sb = sb.tile([P, 1], F32)
         slope_sb = sb.tile([P, 1], F32)
         open_list = sb.tile([P, LIST_COLS], U16)
@@ -60,16 +58,16 @@ def tile_attend_openings_parts_kernel(
         read_list = sb.tile([P, LIST_COLS], U16)
 
         nc.sync.dma_start(out=q2_raw[:], in_=query2.rearrange("(p j) q -> p j q", j=PACK))
-        nc.sync.dma_start(out=q1_raw[:], in_=query.rearrange("(p j) q -> p j q", j=PACK))
-        load_scale_rows(nc.scalar, tag_plane, tags_scales)
+        load_scale_rows(nc.sync, tag_plane, tags_scales)
         nc.sync.dma_start(out=tag_codes[:].bitcast(I32), in_=tags_words[0].bitcast(I32))
-        nc.sync.dma_start(
-            out=key_codes[:].bitcast(I32), in_=keys_words[0].rearrange("p n t -> p (n t)").bitcast(I32)
-        )
-        load_scale_rows(nc.scalar, key_plane, keys_scales)
-        nc.gpsimd.dma_start(out=slope_sb[:], in_=slope)
-        nc.gpsimd.dma_start(out=thr_sb[:], in_=thr)
+        nc.sync.dma_start(out=q1_raw[:], in_=query.rearrange("(p j) q -> p j q", j=PACK))
+        key_rows = keys_words[0].rearrange("p n t -> p (n t)").bitcast(I32)
+        nc.sync.dma_start(out=key_codes[0][:].bitcast(I32), in_=key_rows[:, 0 : T // 2])
+        load_scale_rows(nc.sync, key_plane, keys_scales)
+        nc.sync.dma_start(out=key_codes[1][:].bitcast(I32), in_=key_rows[:, T // 2 : T])
         nc.sync.dma_start(open_list[:], offs)
+        nc.sync.dma_start(out=slope_sb[:], in_=slope)
+        nc.sync.dma_start(out=thr_sb[:], in_=thr)
         nc.sync.dma_start(place_list[:], offs2)
         nc.sync.dma_start(read_list[:], offs3)
 
@@ -85,29 +83,31 @@ def tile_attend_openings_parts_kernel(
             quantised.append((codes, scales))
         (q2_codes, q2_scales), (q1_codes, q1_scales) = quantised
 
-        banks = [psum.tile([P, N], F32, name="bank%d" % b) for b in range(BANKS)]
-        for b in range(BANKS):
+        banks = [psum.tile([P, hi - lo], F32, name="bank%d" % lo) for lo, hi in BANK_COLS]
+        for bank, (lo, hi) in zip(banks, BANK_COLS):
             nc.tensor.matmul_mx(
-                out=banks[b][:],
+                out=bank[:],
                 lhsT=q2_codes[:].bitcast(FP8X4),
                 lhsT_scale=q2_scales[:],
-                rhs=tag_codes[:, 2 * N * b : 2 * N * (b + 1)].bitcast(FP4X4),
-                rhs_scale=tag_plane[:, N * b : N * (b + 1)],
+                rhs=tag_codes[:, 2 * lo : 2 * hi].bitcast(FP4X4),
+                rhs_scale=tag_plane[:, lo:hi],
                 start=True,
                 stop=False,
             )
         scores = sb.tile([P, T], F32)
-        for b in range(BANKS):
+        for b, (lo, hi) in enumerate(BANK_COLS):
+            half, at = divmod(lo, T // 2)
             nc.tensor.matmul_mx(
                 out=banks[b][:],
                 lhsT=q1_codes[:].bitcast(FP8X4),
                 lhsT_scale=q1_scales[:],
-                rhs=key_codes[:, N * b : N * (b + 1)].bitcast(FP8X4),
-                rhs_scale=key_plane[:, N * b : N * (b + 1)],
+                rhs=key_codes[half][:, at : at + hi - lo].bitcast(FP8X4),
+                rhs_scale=key_plane[:, lo:hi],
                 start=False,
                 stop=True,
             )
-            nc.vector.tensor_copy(out=scores[:, N * b : N * (b + 1)], in_=banks[b][:])
+            empty_bank = nc.vector.tensor_copy if b % 2 == 0 else nc.scalar.copy
+            empty_bank(out=scores[:, lo:hi], in_=banks[b][:])
 
         for h in range(2):
             cols = slice(h * HALF_COLS, (h + 1) * HALF_COLS)
@@ -115,10 +115,13 @@ def tile_attend_openings_parts_kernel(
             nc.scalar.activation(
                 opened[:], scores[:].indirect(open_list[:, cols]), ACT.Sigmoid, bias=thr_sb[:], scale=slope_sb[:]
             )
-            nc.vector.tensor_copy(gates[:].indirect(place_list[:, cols]), opened[:])
+            nc.vector.tensor_tensor(gates[:].indirect(place_list[:, cols]), opened[:], opened[:], ALU.add)
 
         gated = sb.tile([P, T], F32)
-        nc.vector.scalar_tensor_tensor(gated[:], gates[:], 2.0, scores[:], ALU.mult, ALU.add)
+        nc.gpsimd.tensor_tensor(gated[:, POOL_FROM:T], gates[:, POOL_FROM:T], scores[:, POOL_FROM:T], ALU.add)
+        for bank, (lo, hi) in zip(banks, BANK_COLS):
+            if hi <= POOL_FROM:
+                nc.vector.tensor_tensor(gated[:, lo:hi], bank[:], gates[:, lo:hi], ALU.add)
 
         first = sb.tile([P, HALF], F32)
         second = sb.tile([P, HALF], F32)

@@ -47,6 +47,11 @@ def tile_attend_openings_parts_kernel(
         gates = sb.tile([P, T], F32)
         nc.vector.memset(gates[:], 0.0)
 
+        warm_in = sb.tile([P, 1], F32)
+        warm_out = sb.tile([P, 1], F32)
+        nc.gpsimd.memset(warm_in[:], 0.0)
+        nc.scalar.activation(warm_out[:], warm_in[:], ACT.Sigmoid)
+
         q2_raw = sb.tile([P, PACK, Q], F32)
         q1_raw = sb.tile([P, PACK, Q], F32)
         tag_codes = sb.tile([P, 2 * T], U8, align_bytes=64)

@@ -19,17 +19,17 @@ ACT = mybir.ActivationFunctionType
 P = 128
 PACK = 4
 BANK_COLS = ((0, 256), (256, 512), (512, 768), (768, 896), (896, 1024))
-POOL_FROM = 768
+KEY_PLANE_ROW = 4
 HALF = SLOTS // 2
 LIST_COLS = SLOTS // 16
 HALF_COLS = LIST_COLS // 2
 
 
-def load_scale_rows(queue, plane, rows):
+def load_scale_rows(queue, plane, rows, first):
     words = rows[0].bitcast(I32)
     for quad in range(4):
         queue.dma_start(
-            out=plane[32 * quad : 32 * quad + 4, :].bitcast(I32),
+            out=plane[32 * quad + first : 32 * quad + first + 4, :].bitcast(I32),
             in_=words[4 * quad : 4 * quad + 4, :],
         )
 
@@ -45,7 +45,7 @@ def tile_attend_openings_parts_kernel(
         tag_plane = sb.tile([P, T], U8, align_bytes=64)
         key_plane = sb.tile([P, T], U8, align_bytes=64)
         gates = sb.tile([P, T], F32)
-        nc.vector.memset(gates[:], 0.0)
+        nc.vector.memset(gates[:].bitcast(I32), 0)
 
         warm_in = sb.tile([P, 1], F32)
         warm_out = sb.tile([P, 1], F32)
@@ -63,16 +63,16 @@ def tile_attend_openings_parts_kernel(
         read_list = sb.tile([P, LIST_COLS], U16)
 
         nc.sync.dma_start(out=q2_raw[:], in_=query2.rearrange("(p j) q -> p j q", j=PACK))
-        load_scale_rows(nc.sync, tag_plane, tags_scales)
+        load_scale_rows(nc.sync, tag_plane, tags_scales, 0)
         nc.sync.dma_start(out=tag_codes[:].bitcast(I32), in_=tags_words[0].bitcast(I32))
         nc.sync.dma_start(out=q1_raw[:], in_=query.rearrange("(p j) q -> p j q", j=PACK))
         key_rows = keys_words[0].rearrange("p n t -> p (n t)").bitcast(I32)
         nc.sync.dma_start(out=key_codes[0][:].bitcast(I32), in_=key_rows[:, 0 : T // 2])
-        load_scale_rows(nc.sync, key_plane, keys_scales)
+        load_scale_rows(nc.sync, key_plane, keys_scales, KEY_PLANE_ROW)
         nc.sync.dma_start(out=key_codes[1][:].bitcast(I32), in_=key_rows[:, T // 2 : T])
-        nc.sync.dma_start(open_list[:], offs)
-        nc.sync.dma_start(out=slope_sb[:], in_=slope)
+        nc.gpsimd.dma_start(out=slope_sb[:], in_=slope)
         nc.sync.dma_start(out=thr_sb[:], in_=thr)
+        nc.sync.dma_start(open_list[:], offs)
         nc.sync.dma_start(place_list[:], offs2)
         nc.sync.dma_start(read_list[:], offs3)
 
@@ -107,11 +107,11 @@ def tile_attend_openings_parts_kernel(
                 lhsT=q1_codes[:].bitcast(FP8X4),
                 lhsT_scale=q1_scales[:],
                 rhs=key_codes[half][:, at : at + hi - lo].bitcast(FP8X4),
-                rhs_scale=key_plane[:, lo:hi],
+                rhs_scale=key_plane[KEY_PLANE_ROW:P, lo:hi],
                 start=False,
                 stop=True,
             )
-            empty_bank = nc.vector.tensor_copy if b % 2 == 0 else nc.scalar.copy
+            empty_bank = nc.scalar.copy if b % 2 == 0 else nc.vector.tensor_copy
             empty_bank(out=scores[:, lo:hi], in_=banks[b][:])
 
         for h in range(2):
@@ -120,13 +120,10 @@ def tile_attend_openings_parts_kernel(
             nc.scalar.activation(
                 opened[:], scores[:].indirect(open_list[:, cols]), ACT.Sigmoid, bias=thr_sb[:], scale=slope_sb[:]
             )
-            nc.vector.tensor_tensor(gates[:].indirect(place_list[:, cols]), opened[:], opened[:], ALU.add)
+            nc.vector.tensor_copy(gates[:].indirect(place_list[:, cols]), opened[:])
 
         gated = sb.tile([P, T], F32)
-        nc.gpsimd.tensor_tensor(gated[:, POOL_FROM:T], gates[:, POOL_FROM:T], scores[:, POOL_FROM:T], ALU.add)
-        for bank, (lo, hi) in zip(banks, BANK_COLS):
-            if hi <= POOL_FROM:
-                nc.vector.tensor_tensor(gated[:, lo:hi], bank[:], gates[:, lo:hi], ALU.add)
+        nc.vector.scalar_tensor_tensor(gated[:], gates[:], 2.0, scores[:], ALU.mult, ALU.add)
 
         first = sb.tile([P, HALF], F32)
         second = sb.tile([P, HALF], F32)

@@ -18,20 +18,20 @@ ACT = mybir.ActivationFunctionType
 
 P = 128
 PACK = 4
+QUADRANT = 32
+SCALE_ROWS = D // 32
 BANK_COLS = ((0, 256), (256, 512), (512, 768), (768, 896), (896, 1024))
-KEY_PLANE_ROW = 4
+KEY_SCALES_FROM = 4
+CAST_SPLIT = 80
 HALF = SLOTS // 2
 LIST_COLS = SLOTS // 16
 HALF_COLS = LIST_COLS // 2
 
 
-def load_scale_rows(queue, plane, rows, first):
+def load_scale_rows(nc, tile, rows, first):
     words = rows[0].bitcast(I32)
-    for quad in range(4):
-        queue.dma_start(
-            out=plane[32 * quad + first : 32 * quad + first + 4, :].bitcast(I32),
-            in_=words[4 * quad : 4 * quad + 4, :],
-        )
+    for r in range(4):
+        nc.sync.dma_start(out=tile[first + r : P : QUADRANT, :].bitcast(I32), in_=words[r:SCALE_ROWS:4, :])
 
 
 def tile_attend_openings_parts_kernel(
@@ -42,8 +42,8 @@ def tile_attend_openings_parts_kernel(
         sb = ctx.enter_context(tc.tile_pool(name="sb", bufs=1))
         psum = ctx.enter_context(tc.psum_pool(name="psum", bufs=1))
 
-        tag_plane = sb.tile([P, T], U8, align_bytes=64)
-        key_plane = sb.tile([P, T], U8, align_bytes=64)
+        tag_scale_tile = sb.tile([P, T], U8, align_bytes=64)
+        key_scale_tile = sb.tile([P, T], U8, align_bytes=64)
         gates = sb.tile([P, T], F32)
         nc.vector.memset(gates[:].bitcast(I32), 0)
 
@@ -63,12 +63,12 @@ def tile_attend_openings_parts_kernel(
         read_list = sb.tile([P, LIST_COLS], U16)
 
         nc.sync.dma_start(out=q2_raw[:], in_=query2.rearrange("(p j) q -> p j q", j=PACK))
-        load_scale_rows(nc.sync, tag_plane, tags_scales, 0)
+        load_scale_rows(nc, tag_scale_tile, tags_scales, 0)
         nc.sync.dma_start(out=tag_codes[:].bitcast(I32), in_=tags_words[0].bitcast(I32))
         nc.sync.dma_start(out=q1_raw[:], in_=query.rearrange("(p j) q -> p j q", j=PACK))
         key_rows = keys_words[0].rearrange("p n t -> p (n t)").bitcast(I32)
         nc.sync.dma_start(out=key_codes[0][:].bitcast(I32), in_=key_rows[:, 0 : T // 2])
-        load_scale_rows(nc.sync, key_plane, keys_scales, KEY_PLANE_ROW)
+        load_scale_rows(nc, key_scale_tile, keys_scales, KEY_SCALES_FROM)
         nc.sync.dma_start(out=key_codes[1][:].bitcast(I32), in_=key_rows[:, T // 2 : T])
         nc.gpsimd.dma_start(out=slope_sb[:], in_=slope)
         nc.sync.dma_start(out=thr_sb[:], in_=thr)
@@ -81,7 +81,9 @@ def tile_attend_openings_parts_kernel(
             grouped = sb.tile([P, Q, PACK], BF16, align_bytes=64, name=name + "_grouped")
             codes = sb.tile([P, Q], U32, align_bytes=64, name=name + "_codes")
             scales = sb.tile([P, Q], U8, align_bytes=64, name=name + "_scales")
-            nc.vector.tensor_copy(out=grouped[:], in_=raw[:].rearrange("p j q -> p q j"))
+            turned = raw[:].rearrange("p j q -> p q j")
+            nc.vector.tensor_copy(out=grouped[:, 0:CAST_SPLIT, :], in_=turned[:, 0:CAST_SPLIT, :])
+            nc.scalar.copy(out=grouped[:, CAST_SPLIT:Q, :], in_=turned[:, CAST_SPLIT:Q, :])
             nc.vector.quantize_mx(
                 out=codes[:].bitcast(FP8X4), scales=scales[:], in_=grouped[:].rearrange("p q j -> p (q j)")
             )
@@ -95,7 +97,7 @@ def tile_attend_openings_parts_kernel(
                 lhsT=q2_codes[:].bitcast(FP8X4),
                 lhsT_scale=q2_scales[:],
                 rhs=tag_codes[:, 2 * lo : 2 * hi].bitcast(FP4X4),
-                rhs_scale=tag_plane[:, lo:hi],
+                rhs_scale=tag_scale_tile[:, lo:hi],
                 start=True,
                 stop=False,
             )
@@ -107,7 +109,7 @@ def tile_attend_openings_parts_kernel(
                 lhsT=q1_codes[:].bitcast(FP8X4),
                 lhsT_scale=q1_scales[:],
                 rhs=key_codes[half][:, at : at + hi - lo].bitcast(FP8X4),
-                rhs_scale=key_plane[KEY_PLANE_ROW:P, lo:hi],
+                rhs_scale=key_scale_tile[KEY_SCALES_FROM:P, lo:hi],
                 start=False,
                 stop=True,
             )
@@ -125,9 +127,9 @@ def tile_attend_openings_parts_kernel(
         gated = sb.tile([P, T], F32)
         nc.vector.scalar_tensor_tensor(gated[:], gates[:], 2.0, scores[:], ALU.mult, ALU.add)
 
-        first = sb.tile([P, HALF], F32)
-        second = sb.tile([P, HALF], F32)
-        nc.vector.tensor_copy(first[:], gated[:].indirect(read_list[:, 0:HALF_COLS]))
-        nc.scalar.activation(second[:], gated[:].indirect(read_list[:, HALF_COLS:LIST_COLS]), ACT.Copy)
-        nc.sync.dma_start(out=out[:, 0:HALF], in_=first[:])
-        nc.scalar.dma_start(out=out[:, HALF:SLOTS], in_=second[:])
+        out_low = sb.tile([P, HALF], F32)
+        out_high = sb.tile([P, HALF], F32)
+        nc.vector.tensor_copy(out_low[:], gated[:].indirect(read_list[:, 0:HALF_COLS]))
+        nc.scalar.activation(out_high[:], gated[:].indirect(read_list[:, HALF_COLS:LIST_COLS]), ACT.Copy)
+        nc.sync.dma_start(out=out[:, 0:HALF], in_=out_low[:])
+        nc.scalar.dma_start(out=out[:, HALF:SLOTS], in_=out_high[:])

from contextlib import ExitStack

import concourse.mybir as mybir

D, T, SLOTS, Q = 512, 1024, 512, 128
FLOPS = 2 * 2 * D * Q * T

F32 = mybir.dt.float32
BF16 = mybir.dt.bfloat16
I32 = mybir.dt.int32
U32 = mybir.dt.uint32
U16 = mybir.dt.uint16
U8 = mybir.dt.uint8
FP8X4 = mybir.dt.float8_e4m3fn_x4
FP4X4 = mybir.dt.float4_e2m1fn_x4
ALU = mybir.AluOpType
ACT = mybir.ActivationFunctionType

P = 128
PACK = 4
QUADRANT = 32
SCALE_ROWS = D // 32
BANK_COLS = ((0, 256), (256, 512), (512, 768), (768, 896), (896, 1024))
KEY_SCALES_FROM = 4
CAST_SPLIT = 80
HALF = SLOTS // 2
LIST_COLS = SLOTS // 16
HALF_COLS = LIST_COLS // 2


def load_scale_rows(nc, tile, rows, first):
    words = rows[0].bitcast(I32)
    for r in range(4):
        nc.sync.dma_start(out=tile[first + r : P : QUADRANT, :].bitcast(I32), in_=words[r:SCALE_ROWS:4, :])


def tile_attend_openings_parts_kernel(
    tc, query, query2, keys_words, keys_scales, tags_words, tags_scales, thr, slope, offs, offs2, offs3, out
):
    nc = tc.nc
    with ExitStack() as ctx:
        sb = ctx.enter_context(tc.tile_pool(name="sb", bufs=1))
        psum = ctx.enter_context(tc.psum_pool(name="psum", bufs=1))

        tag_scale_tile = sb.tile([P, T], U8, align_bytes=64)
        key_scale_tile = sb.tile([P, T], U8, align_bytes=64)
        gates = sb.tile([P, T], F32)
        nc.vector.memset(gates[:].bitcast(I32), 0)

        warm_in = sb.tile([P, 1], F32)
        warm_out = sb.tile([P, 1], F32)
        nc.gpsimd.memset(warm_in[:], 0.0)
        nc.scalar.activation(warm_out[:], warm_in[:], ACT.Sigmoid)

        q2_raw = sb.tile([P, PACK, Q], F32)
        q1_raw = sb.tile([P, PACK, Q], F32)
        tag_codes = sb.tile([P, 2 * T], U8, align_bytes=64)
        key_codes = [sb.tile([P, T // 2], U32, align_bytes=64, name="key_codes%d" % h) for h in range(2)]
        thr_sb = sb.tile([P, 1], F32)
        slope_sb = sb.tile([P, 1], F32)
        open_list = sb.tile([P, LIST_COLS], U16)
        place_list = sb.tile([P, LIST_COLS], U16)
        read_list = sb.tile([P, LIST_COLS], U16)

        nc.sync.dma_start(out=q2_raw[:], in_=query2.rearrange("(p j) q -> p j q", j=PACK))
        load_scale_rows(nc, tag_scale_tile, tags_scales, 0)
        nc.sync.dma_start(out=tag_codes[:].bitcast(I32), in_=tags_words[0].bitcast(I32))
        nc.sync.dma_start(out=q1_raw[:], in_=query.rearrange("(p j) q -> p j q", j=PACK))
        key_rows = keys_words[0].rearrange("p n t -> p (n t)").bitcast(I32)
        nc.sync.dma_start(out=key_codes[0][:].bitcast(I32), in_=key_rows[:, 0 : T // 2])
        load_scale_rows(nc, key_scale_tile, keys_scales, KEY_SCALES_FROM)
        nc.sync.dma_start(out=key_codes[1][:].bitcast(I32), in_=key_rows[:, T // 2 : T])
        nc.gpsimd.dma_start(out=slope_sb[:], in_=slope)
        nc.sync.dma_start(out=thr_sb[:], in_=thr)
        nc.sync.dma_start(open_list[:], offs)
        nc.sync.dma_start(place_list[:], offs2)
        nc.sync.dma_start(read_list[:], offs3)

        quantised = []
        for name, raw in (("q2", q2_raw), ("q1", q1_raw)):
            grouped = sb.tile([P, Q, PACK], BF16, align_bytes=64, name=name + "_grouped")
            codes = sb.tile([P, Q], U32, align_bytes=64, name=name + "_codes")
            scales = sb.tile([P, Q], U8, align_bytes=64, name=name + "_scales")
            turned = raw[:].rearrange("p j q -> p q j")
            nc.vector.tensor_copy(out=grouped[:, 0:CAST_SPLIT, :], in_=turned[:, 0:CAST_SPLIT, :])
            nc.scalar.copy(out=grouped[:, CAST_SPLIT:Q, :], in_=turned[:, CAST_SPLIT:Q, :])
            nc.vector.quantize_mx(
                out=codes[:].bitcast(FP8X4), scales=scales[:], in_=grouped[:].rearrange("p q j -> p (q j)")
            )
            quantised.append((codes, scales))
        (q2_codes, q2_scales), (q1_codes, q1_scales) = quantised

        banks = [psum.tile([P, hi - lo], F32, name="bank%d" % lo) for lo, hi in BANK_COLS]
        for bank, (lo, hi) in zip(banks, BANK_COLS):
            nc.tensor.matmul_mx(
                out=bank[:],
                lhsT=q2_codes[:].bitcast(FP8X4),
                lhsT_scale=q2_scales[:],
                rhs=tag_codes[:, 2 * lo : 2 * hi].bitcast(FP4X4),
                rhs_scale=tag_scale_tile[:, lo:hi],
                start=True,
                stop=False,
            )
        scores = sb.tile([P, T], F32)
        for b, (lo, hi) in enumerate(BANK_COLS):
            half, at = divmod(lo, T // 2)
            nc.tensor.matmul_mx(
                out=banks[b][:],
                lhsT=q1_codes[:].bitcast(FP8X4),
                lhsT_scale=q1_scales[:],
                rhs=key_codes[half][:, at : at + hi - lo].bitcast(FP8X4),
                rhs_scale=key_scale_tile[KEY_SCALES_FROM:P, lo:hi],
                start=False,
                stop=True,
            )
            empty_bank = nc.scalar.copy if b % 2 == 0 else nc.vector.tensor_copy
            empty_bank(out=scores[:, lo:hi], in_=banks[b][:])

        for h in range(2):
            cols = slice(h * HALF_COLS, (h + 1) * HALF_COLS)
            opened = sb.tile([P, HALF], F32, name="opened%d" % h)
            nc.scalar.activation(
                opened[:], scores[:].indirect(open_list[:, cols]), ACT.Sigmoid, bias=thr_sb[:], scale=slope_sb[:]
            )
            nc.vector.tensor_copy(gates[:].indirect(place_list[:, cols]), opened[:])

        gated = sb.tile([P, T], F32)
        nc.vector.scalar_tensor_tensor(gated[:], gates[:], 2.0, scores[:], ALU.mult, ALU.add)

        out_low = sb.tile([P, HALF], F32)
        out_high = sb.tile([P, HALF], F32)
        nc.vector.tensor_copy(out_low[:], gated[:].indirect(read_list[:, 0:HALF_COLS]))
        nc.scalar.activation(out_high[:], gated[:].indirect(read_list[:, HALF_COLS:LIST_COLS]), ACT.Copy)
        nc.sync.dma_start(out=out[:, 0:HALF], in_=out_low[:])
        nc.scalar.dma_start(out=out[:, HALF:SLOTS], in_=out_high[:])
